import numpy as np, ml_dtypes
CORES = [37,45,53,61,69,109,117,125]
N = 8
T, EL, CAP, CAPP = 2048, 4, 480, 128
E = N * EL
def entries(a): return a.T.reshape(-1)
def pack(v, P): return np.ascontiguousarray(np.asarray(v, np.int32).reshape(-1, P).T)
def lists(rng, how):
    if how == "uniform": return {"ex": np.stack([pack(rng.permutation(np.repeat(np.arange(E), CAPP))[:T], 16) for r in range(N)])}
    R = np.arange(N)[:, None]; c = rng.permutation(E); C = np.zeros((N, E), np.int64)
    if how == "bands":
        a = c % N; C = CAPP * ((R >= a) & (R <= a + CAP // CAPP)); C[a, np.arange(E)] = np.where(c < N, CAPP, rng.integers(1, CAPP + 1, E))
    if how == "full":
        g = T // CAPP; C[:, c[:g]] = CAPP; C[:, c[:g // 2]] = rng.integers(CAPP // 2, CAPP + 1, (N, g // 2))
    if how in ("skew", "sorted"):
        V = np.full((N, 3), CAP // N); V[:, 0] = rng.integers(2, CAP // N + 1, N); h = rng.integers(1, N - 2); V[h, 0] = 0; V[h + 1, 0] = 1; V[rng.integers(N), 1:] += CAP % N; V[rng.integers(N), 2] += 1
        W = rng.random((N, E)) ** 4 + 1e-9; W[:, c[:3]] = 0
        C = np.minimum(((T - T // 8 - V.sum(axis=1, keepdims=True)) * W / W.sum(axis=1, keepdims=True)).astype(np.int64), CAPP); C[:, c[:3]] = V
    if how == "thin":
        C = rng.integers(0, CAP // N + 1, (N, E)); C[1] = 1; C[[0, N // 2, N - 1]] = 0
    X = np.stack([rng.permutation(np.concatenate([np.repeat(np.arange(E), C[r]), np.full(T - C[r].sum(), -1)])) for r in range(N)])
    if how == "sorted": X = np.sort(X, axis=1); X[1::2] = X[1::2, ::-1].copy()
    return {"ex": np.stack([pack(v, 16) for v in X])}
def blank(d):
    for r in range(0, N, 2):
        u, i = np.unique(entries(d["ex"][r])[::-1], return_index=True); d["x"][r][:, T - 1 - i[u >= 0]] = 0
def setup_inputs(rng):
    return dict({"x": rng.standard_normal((N, 128, T), dtype=np.float32).astype(ml_dtypes.bfloat16)}, **lists(rng, "uniform"))
def setup_inputs_bands(rng):
    d = setup_inputs(rng); d.update(lists(rng, "bands"))
    for k in ("x",): d[k] = (d[k].astype(np.float32) * 1048576.0).astype(d[k].dtype)
    blank(d)
    return d
def setup_inputs_full(rng):
    d = setup_inputs(rng); d.update(lists(rng, "full"))
    for k in ("x",): d[k] = (d[k].astype(np.float32) * (1 / 1024.0)).astype(d[k].dtype)
    blank(d)
    return d
def setup_inputs_skew(rng):
    d = setup_inputs(rng); d.update(lists(rng, "skew"))
    blank(d)
    return d
def setup_inputs_sorted(rng):
    d = setup_inputs(rng); d.update(lists(rng, "sorted"))
    blank(d)
    return d
def setup_inputs_thin(rng):
    d = setup_inputs(rng); d.update(lists(rng, "thin"))
    blank(d)
    return d
def check_inputs(x):
    bad = []
    if x["ex"].min() < -1 or x["ex"].max() >= E: bad.append("ex out of range")
    if max(int(np.bincount(entries(a)[entries(a) >= 0], minlength=E).max()) for a in x["ex"]) > CAPP: bad.append("more than CAPP tokens of one rank choose one expert")
    return bad
def reference(x, ex):
    X = np.concatenate(list(x), axis=1); e = np.concatenate([entries(a) for a in ex])
    k = np.nonzero(e >= 0)[0]; o = k[np.argsort(e[k], kind="stable")]; s = e[o]
    p = np.arange(len(o)) - np.searchsorted(s, s)
    Y = np.zeros((128, E * CAP), x.dtype); m = p < CAP; Y[:, CAP * s[m] + p[m]] = X[:, o[m]]
    return {"y": np.stack([Y[:, EL * CAP * r:EL * CAP * (r + 1)] for r in range(N)])}

@@ -1,0 +1,363 @@
+from concourse.bass import DstId, RemoteDMATransfer
+from concourse.mybir import AluOpType as A, ActivationFunctionType as F
+
+N, TOK, EL, CAP, CAPP = 8, 2048, 4, 480, 128
+BLK = EL * CAPP
+ZERO = N * BLK
+NZ = (EL - 1) * CAPP + CAP
+NP = CAP // 16
+
+SCRATCH = {
+    "exi": ("sbuf", [128, 128], "int32"),
+    "xs": ("sbuf", [128, TOK], "bfloat16"),
+    "recv": ("sbuf", [128, ZERO + NZ], "bfloat16"),
+    "win": ("sbuf", [128, 2048 + 256], "bfloat16"),
+    "ci": ("sbuf", [128, 4], "int32"),
+    "cf": ("sbuf", [128, 4], "float32"),
+    "cd": ("sbuf", [128, 16], "float32"),
+    "ebase": ("sbuf", [128, 2], "float32"),
+    "colg": ("sbuf", [128, 128], "bfloat16"),
+    "colp": ("sbuf", [128, 256], "bfloat16"),
+    "n16": ("sbuf", [128, NP], "float32"),
+    "jnum": ("sbuf", [128, 256], "bfloat16"),
+    "vals": ("sbuf", [128, 256], "bfloat16"),
+    "mb": ("sbuf", [128, 128], "bfloat16"),
+    "mgt": ("sbuf", [128, 128], "bfloat16"),
+    "ml": ("sbuf", [128, 128], "bfloat16"),
+    "mr": ("sbuf", [128, 128], "bfloat16"),
+    "mz": ("sbuf", [128, 144], "bfloat16"),
+    "me": ("sbuf", [128, 256], "bfloat16"),
+    "njl": ("sbuf", [128, 128], "bfloat16"),
+    "jt": ("sbuf", [128, 16], "bfloat16"),
+    "dm": ("sbuf", [128, 8], "bfloat16"),
+    "off": ("sbuf", [128, 16], "uint16"),
+    "ct": ("sbuf", [4, 256], "bfloat16"),
+    "cb": ("dram", [4, 128, 2], "bfloat16"),
+    "rcnt": ("dram", [N, 128, 2], "bfloat16"),
+    "cnts": ("sbuf", [128, 16], "bfloat16"),
+    "mge": ("sbuf", [128, 128], "bfloat16"),
+    "mcum": ("sbuf", [128, 128], "bfloat16"),
+    "mrf": ("sbuf", [128, 128], "float32"),
+    "pcmp": ("sbuf", [128, NP], "float32"),
+    "pbase": ("sbuf", [128, EL * NP], "float32"),
+    "wgt": ("sbuf", [128, EL], "float32"),
+    "ff": ("sbuf", [128, EL * NP], "float32"),
+    "ylist": ("sbuf", [128, EL * NP], "uint16"),
+    "yt": ("sbuf", [128, EL * CAP], "bfloat16"),
+    "pq": ("psum", [128, 512], "float32"),
+    "pc": ("psum", [128, 512], "float32"),
+    "pcum": ("psum", [128, 512], "float32"),
+    "plr": ("psum", [128, 512], "float32"),
+}
+for _k in range(2):
+    SCRATCH["oh%d" % _k] = ("sbuf", [128, 128], "bfloat16")
+    SCRATCH["rc%d" % _k] = ("sbuf", [128, 136], "bfloat16")
+    SCRATCH["v%d" % _k] = ("sbuf", [128, 128], "bfloat16")
+    SCRATCH["rs%d" % _k] = ("sbuf", [128, 16], "bfloat16")
+    SCRATCH["rh%d" % _k] = ("sbuf", [128, 256], "bfloat16")
+    SCRATCH["list%d" % _k] = ("sbuf", [128, 64], "uint16")
+    SCRATCH["pp%d" % _k] = ("psum", [128, 512], "float32")
+    SCRATCH["pl%d" % _k] = ("psum", [128, 512], "float32")
+for _k in range(4):
+    SCRATCH["sb%d" % _k] = ("sbuf", [128, BLK], "bfloat16")
+
+NEV = 64
+SEMAPHORES = ["exs", "xa", "xb", "xin", "cbs", "own", "cin", "cld", "arr", "ls", "ysa", "ysb"] + ["e%d" % i for i in range(NEV)]
+
+
+def engines(mask):
+    return [1 << b for b in range(mask.bit_length()) if (mask >> b) & 1]
+
+
+def plan(r, cores, topo):
+    me = cores[r]
+    order = [(r + i) % N for i in range(1, N)]
+    direct = [d for d in order if topo.may_write(me, cores[d])]
+    other = [d for d in order if not topo.may_write(me, cores[d])]
+    chip = topo.chip(me)
+    helpers = [c for c in range(128) if topo.chip(c) == chip and topo.die(c) != topo.die(me)
+               and all(topo.may_write(c, cores[d]) for d in other)]
+    return [(me, direct + [r]), (helpers[0], other[:2]), (helpers[1], other[2:])]
+
+
+def count_engines(w, r):
+    remote = [d for d in w[1] if d != r]
+    return 4 if len(remote) <= 2 else 2
+
+
+def rank_program(g, core, T, topo):
+    cores = list(T.cores)
+    mine = [q for q in range(N) if topo.chip(cores[q]) == topo.chip(core)]
+    if not mine:
+        return
+    r = mine[0]
+    workers = plan(r, cores, topo)
+    me = [w for w in workers if w[0] == core]
+    if not me:
+        return
+    w = me[0]
+    dests = w[1]
+    is_rank = core == cores[r]
+    helpers = [h[0] for h in workers[1:]]
+    nd = len(dests)
+    K = nd // 2
+    TB = 1024 * K
+    V, S, P, Y = g.vector, g.scalar, g.tensor, g.sync
+    used = [0]
+    local = [0]
+    seen = {}
+
+    def group():
+        used[0] += 1
+        return {"sem": T.sem["e%d" % (used[0] - 1)], "n": 0, "key": used[0]}
+
+    def add(grp, inst):
+        inst.then_inc(grp["sem"], 1)
+        grp["n"] += 1
+
+    def one(inst):
+        grp = group()
+        add(grp, inst)
+        return grp
+
+    def wait(name, q, *grps):
+        for grp in grps:
+            if (name, grp["key"]) in seen:
+                continue
+            seen[(name, grp["key"])] = True
+            q.wait_ge(grp["sem"], grp["n"])
+
+    def send(dst, out, in_, rsem, mask):
+        rid, pid, _s = topo.addr(dst)
+        g.remote_dma(out, in_, rsem, T.sem.ls, pid, rid, mask)
+        local[0] += len(engines(mask))
+
+    def send_fused(parts, rsem):
+        tr = []
+        for dst, out, in_, eng in parts:
+            rid, pid, _s = topo.addr(dst)
+            tr.append(RemoteDMATransfer(dst_ids=[DstId(rid=rid, pnc=pid)], dma_engine_mask=sum(eng), remote_sem=rsem,
+                                        src=in_, dst=out))
+            local[0] += len(eng)
+        g.remote_dma_fused(tr, local_sem=T.sem.ls)
+
+    half = TOK // 2
+    onchip = engines(topo.mask(core, helpers[0])) if is_rank else []
+    if is_rank:
+        for q in range(4):
+            Y.dma_start(T.exi[16 * q:16 * q + 16, :], T.ex[:, :]).then_inc(T.sem.exs, 16)
+            S.dma_start(T.exi[64 + 16 * q:80 + 16 * q, :], T.ex[:, :]).then_inc(T.sem.exs, 16)
+        Y.dma_start(T.xs[:, 0:half], T.x[:, 0:half]).then_inc(T.sem.xa, 16)
+        S.dma_start(T.xs[:, half:TOK], T.x[:, half:TOK]).then_inc(T.sem.xb, 16)
+        exw = {"sem": T.sem.exs, "n": 128, "key": "ex"}
+        xw = [{"sem": T.sem.xa, "n": 16, "key": "xa"}, {"sem": T.sem.xb, "n": 16, "key": "xb"}]
+    else:
+        exw = {"sem": T.sem.exs, "n": 8, "key": "ex"}
+        first = core == helpers[0]
+        nx = len(engines(topo.mask(cores[r], core)))
+        xw = [{"sem": T.sem.xin, "n": nx * (2 if first else 1), "key": "xin"}]
+
+    it_row = one(g.iota(T.ci[:, 0:1], [[0, 1]], 0, 1))
+    it_cp = one(g.iota(T.colp[:, :], [[0, 16], [1, 16]], 0, 0, allow_small_or_imprecise_dtypes=True))
+    it_cg = one(g.iota(T.colg[:, :], [[1, 8], [0, 16]], 0, 0, allow_small_or_imprecise_dtypes=True))
+    it_jn = group()
+    add(it_jn, g.iota(T.n16[:, :], [[16, NP]], 0, 0, allow_small_or_imprecise_dtypes=True))
+    add(it_jn, g.iota(T.jnum[:, :], [[1, 16], [16, 16]], 0, 0, allow_small_or_imprecise_dtypes=True))
+    if is_rank:
+        wait("g", g, exw)
+        send_fused([(helpers[i], T.exi[:, :], T.exi[:, :], onchip[8 * i:8 * i + 8]) for i in range(2)], T.sem.exs)
+        wait("g", g, xw[0])
+        send(helpers[0], T.xs[:, 0:half], T.xs[:, 0:half], T.sem.xin, sum(onchip))
+        wait("g", g, xw[1])
+        send(helpers[0], T.xs[:, half:TOK], T.xs[:, half:TOK], T.sem.xin, sum(onchip))
+        send(helpers[1], T.xs[:, :], T.xs[:, :], T.sem.xin, sum(onchip))
+        it_pb = one(g.iota(T.pbase[0:16, :], [[CAPP, EL], [16, NP]], 0, 1, allow_small_or_imprecise_dtypes=True))
+
+    rg, rp, g4 = T.cf[:, 1:2], T.cf[:, 2:3], T.cf[:, 3:4]
+
+    def cd(i):
+        return T.cd[:, i:i + 1]
+    m0 = group()
+    for k in range(K):
+        add(m0, V.memset(T["rc%d" % k][:, 0:8], 0.0))
+        add(m0, V.memset(T.ebase[0:64, k:k + 1], float(EL * dests[2 * k])))
+        add(m0, V.memset(T.ebase[64:128, k:k + 1], float(EL * dests[2 * k + 1])))
+    add(m0, V.memset(T.dm[:, 0:nd * K], 0.0))
+    wz = group()
+    vz = 512 if is_rank else TB
+    add(wz, V.memset(T.win[:, 0:vz], 0.0))
+    for c in range(vz, TB, 256):
+        wait("S", S, it_cp)
+        add(wz, S.activation(T.win[:, c:c + 256], T.colp[:, :], F.Copy, scale=0.0))
+    wait("V", V, it_row)
+    s1 = group()
+    add(s1, V.tensor_scalar(T.ci[:, 1:2], T.ci[:, 0:1], 4, None, A.arith_shift_right))
+    add(s1, V.tensor_scalar(T.ci[:, 2:3], T.ci[:, 0:1], 15, None, A.bitwise_and))
+    add(s1, V.tensor_scalar(T.ci[:, 3:4], T.ci[:, 0:1], 4, 3, A.arith_shift_right, A.bitwise_and))
+    wait("V", V, s1)
+    s2 = one(V.tensor_copy(T.cf[:, :], T.ci[:, :]))
+    wait("V", V, s2, m0)
+    s3 = group()
+    for k in range(K):
+        add(s3, V.tensor_scalar(cd(6 + k), T.ebase[:, k:k + 1], g4, None, A.add))
+    add(s3, V.tensor_scalar(cd(0), rp, -16.0, None, A.mult))
+    s5 = group()
+    add(s5, V.tensor_scalar(cd(1), rp, 0.0, None, A.is_equal))
+    add(s5, V.tensor_scalar(cd(8), rp, 0.0, None, A.is_gt))
+    add(s5, V.tensor_scalar(cd(2), rp, 1.0, rg, A.is_equal, A.mult))
+    for k in range(K):
+        add(s5, V.tensor_scalar(cd(4 + k), rg, 128.0, float(1024 * k - TB), A.mult, A.add))
+    dmg = group()
+    for k in range(K):
+        add(dmg, V.memset(T.dm[0:64, nd * k + 2 * k:nd * k + 2 * k + 1], 1.0))
+        add(dmg, V.memset(T.dm[64:128, nd * k + 2 * k + 1:nd * k + 2 * k + 2], 1.0))
+    wait("V", V, it_cp)
+    gt = one(V.tensor_scalar(T.mgt[:, :], T.colp[:, 0:128], rp, None, A.is_gt))
+    mr = one(V.tensor_scalar(T.mr[:, :], T.colp[:, 0:128], rp, None, A.is_equal))
+    wait("V", V, s3)
+    njl = one(V.tensor_scalar(T.njl[:, :], T.colp[:, 0:128], -1.0, cd(0), A.mult, A.add))
+    me = one(V.tensor_scalar(T.me[:, :], T.colp[:, :], g4, None, A.is_equal))
+    wait("V", V, it_cg)
+    mb = one(V.tensor_scalar(T.mb[:, :], T.colg[:, :], rg, None, A.is_equal))
+    wait("V", V, mb, gt)
+    ml = one(V.tensor_tensor(T.ml[:, :], T.mgt[:, :], T.mb[:, :], A.mult))
+
+    wait("V", V, exw)
+    oh, sc, pl = [], [], []
+    for k in range(K):
+        oh.append(one(V.tensor_scalar(T["oh%d" % k][:, :], T.exi[:, :], cd(6 + k), None, A.is_equal)))
+    for k in range(K):
+        wait("V", V, oh[k])
+        o = T["oh%d" % k]
+        sc.append(one(V.tensor_tensor_scan(T["rc%d" % k][:, 8:136], o[:, :], o[:, :], 0.0, A.add, A.max)))
+    wait("P", P, mr, njl)
+    for k in range(K):
+        P.matmul(T["pp%d" % k][:, 0:128], T.mr[0:16, :], T.njl[0:16, :], True, False)
+    wait("P", P, mb, ml, m0)
+    for k in range(K):
+        o, c, pp = T["oh%d" % k], T["rc%d" % k], T["pp%d" % k]
+        wait("P", P, oh[k])
+        P.matmul(pp[:, 0:128], T.ml[:, :], o[:, :], False, False)
+        wait("P", P, sc[k])
+        pl.append(one(P.matmul(pp[:, 0:128], T.mb[:, :], c[:, 7:135], False, True)))
+    wait("V", V, it_jn, mr, s5)
+    jt = group()
+    add(jt, V.tensor_scalar(T.jt[:, :], T.n16[:, 0:16], rp, None, A.add))
+    for k in range(K):
+        add(jt, V.tensor_scalar(T["rs%d" % k][:, :], T.colp[:, 0:16], rp, cd(4 + k), A.is_equal, A.mult))
+    wait("V", V, me)
+    rh = group()
+    for k in range(K):
+        wait("V", V, sc[k])
+        add(rh, V.tensor_scalar(T["rh%d" % k][:, :], T.me[:, :], T["rc%d" % k][:, 135:136], None, A.mult))
+    mul = []
+    for k in range(K):
+        wait("V", V, pl[k])
+        mul.append(one(V.tensor_tensor(T["v%d" % k][:, :], T["pp%d" % k][:, 0:128], T["oh%d" % k][:, :], A.mult)))
+    wait("P", P, jt)
+    P.matmul(T.pq[:, 0:16], T.mr[0:16, :], T.jt[0:16, :], True, False)
+    for k in range(K):
+        P.matmul(T.pq[:, 0:16], T["oh%d" % k][:, :], T["rs%d" % k][:, :], False, False)
+    for k in range(K):
+        wait("P", P, mul[k])
+        inst = P.matmul(T.pq[:, 0:16], T["v%d" % k][:, :], T.mr[:, 0:16], False, k == K - 1)
+    qd = one(inst)
+    wt = one(V.tensor_scalar(cd(3), cd(2), 256.0, cd(1), A.mult, A.add))
+    va = one(V.tensor_scalar(T.vals[:, :], T.jnum[:, :], cd(1), cd(8), A.mult, A.add))
+    wait("V", V, wt)
+    mz = one(V.tensor_scalar(T.mz[:, :], T.colp[:, 0:144], 15.0, cd(3), A.is_equal, A.mult))
+    wait("V", V, qd)
+    of = one(V.tensor_scalar(T.off[:, :], T.pq[:, 0:16], float(TB), None, A.add))
+    wait("V", V, of, va, wz)
+    scat = one(V.tensor_copy(T.win[:, 0:TB + 256].indirect(T.off[:, 0:16]), T.vals[:, :]))
+    wait("P", P, dmg, rh)
+    for k in range(K):
+        inst = P.matmul(T.pc[0:nd, 0:256], T.dm[:, nd * k:nd * k + nd], T["rh%d" % k][:, :], k == 0, k == K - 1)
+    pc = one(inst)
+    wait("S", S, pc)
+    ctd = one(S.activation(T.ct[0:nd, :], T.pc[0:nd, 0:256], F.Copy))
+    remote = [d for d in dests if d != r]
+    nr = len(remote)
+    wait("Y", Y, ctd)
+    Y.dma_start(T.cb[0:nr], T.ct[0:nr, :]).then_inc(T.sem.cbs, 16)
+    if is_rank:
+        Y.dma_start(T.rcnt[r], T.ct[nr:nd, :]).then_inc(T.sem.own, 16)
+    wait("P", P, scat, mz)
+    ll = []
+    for k in range(K):
+        for m in range(16):
+            inst = P.matmul(T["pl%d" % k][:, 0:64], T.mz[:, 15 - m:143 - m], T.win[:, 1024 * k + m:1024 * (k + 1):16],
+                            m == 0, m == 15)
+        ll.append(one(inst))
+    blk = []
+    for k in range(K):
+        wait("V", V, ll[k])
+        lk = one(V.tensor_copy(T["list%d" % k][:, :], T["pl%d" % k][:, 0:64]))
+        wait("V", V, lk, *xw)
+        wait("S", S, lk, *xw)
+        for h in range(2):
+            di = 2 * k + h
+            out = T.recv[:, r * BLK:(r + 1) * BLK] if dests[di] == r else T["sb%d" % di][:, :]
+            src = T.xs[:, :].indirect(T["list%d" % k][:, 32 * h:32 * h + 32])
+            blk.append(one(V.tensor_copy(out, src) if h == 0 else S.activation(out, src, F.Copy)))
+    ne = count_engines(w, r)
+    wait("g", g, {"sem": T.sem.cbs, "n": 16, "key": "cbs"})
+    parts = []
+    for i, d in enumerate(remote):
+        eng = engines(topo.mask(core, cores[d]))
+        parts.append((cores[d], T.rcnt[r], T.cb[i], eng[ne * i:ne * i + ne]))
+    send_fused(parts, T.sem.cin)
+    for i, d in enumerate(remote):
+        wait("g", g, blk[i])
+        send(cores[d], T.recv[:, r * BLK:(r + 1) * BLK], T["sb%d" % i][:, :], T.sem.arr, topo.mask(core, cores[d]))
+    if is_rank:
+        zz = one(V.memset(T.recv[:, ZERO:ZERO + NZ], 0.0))
+        ge = one(V.tensor_scalar(T.mge[:, :], T.colg[:, :], rg, None, A.is_ge))
+        mrf = one(V.tensor_copy(T.mrf[:, :], T.mr[:, :]))
+        pcm = one(V.tensor_scalar(T.pcmp[:, :], T.n16[:, :], rp, None, A.add))
+        wait("V", V, ge)
+        cm = one(V.tensor_tensor(T.mcum[:, :], T.mge[:, :], T.mr[:, :], A.mult))
+        ncin = narr = 0
+        for q in range(N):
+            if q == r:
+                continue
+            for v in plan(q, cores, topo):
+                if r in v[1]:
+                    ncin += count_engines(v, q)
+                    narr += len(engines(topo.mask(v[0], core)))
+        Y.wait_ge(T.sem.own, 16)
+        Y.wait_ge(T.sem.cin, ncin)
+        Y.dma_start(T.cnts[:, :], T.rcnt[:]).then_inc(T.sem.cld, 16)
+        cl = {"sem": T.sem.cld, "n": 16, "key": "cld"}
+        wait("P", P, it_pb, mrf)
+        P.matmul(T.plr[:, 0:EL * NP], T.mrf[0:16, :], T.pbase[0:16, :], True, False)
+        wait("P", P, cl, cm)
+        cum = one(P.matmul(T.pcum[:, 0:EL], T.mcum[:, :], T.cnts[:, 0:EL], True, True))
+        wait("V", V, cl)
+        wg = one(V.tensor_scalar(T.wgt[:, :], T.cnts[:, 0:EL], -1.0, float(BLK), A.mult, A.add))
+        wait("V", V, cum, wg, pcm)
+        ff = group()
+        for e in range(EL):
+            add(ff, V.tensor_scalar(T.ff[:, NP * e:NP * e + NP], T.pcmp[:, :], T.pcum[:, e:e + 1], T.wgt[:, e:e + 1],
+                                    A.is_ge, A.mult))
+        wait("P", P, ff)
+        lr = one(P.matmul(T.plr[:, 0:EL * NP], T.mrf[:, :], T.ff[:, :], False, True))
+        wait("V", V, lr)
+        yl = one(V.tensor_copy(T.ylist[:, :], T.plr[:, 0:EL * NP]))
+        ar = {"sem": T.sem.arr, "n": narr, "key": "arr"}
+        wait("V", V, yl, ar, zz, blk[nd - 1])
+        wait("S", S, yl, ar, zz, blk[nd - 1])
+        yo = {}
+        for i in range(2):
+            for q, e in ((0, i), (1, 2 + i)):
+                src = T.recv[:, :].indirect(T.ylist[:, NP * e:NP * e + NP])
+                out = T.yt[:, CAP * e:CAP * e + CAP]
+                yo[e] = one(V.tensor_copy(out, src) if q == 0 else S.activation(out, src, F.Copy))
+        for e in (0, 2, 1):
+            wait("Y", Y, yo[e])
+            Y.dma_start(T.y[:, CAP * e:CAP * e + CAP], T.yt[:, CAP * e:CAP * e + CAP]).then_inc(T.sem.ysa, 16)
+        wait("S", S, yo[3])
+        S.dma_start(T.y[:, 3 * CAP:4 * CAP], T.yt[:, 3 * CAP:4 * CAP]).then_inc(T.sem.ysb, 16)
+        Y.wait_ge(T.sem.ysa, 48)
+        S.wait_ge(T.sem.ysb, 16)
+    g.wait_ge(T.sem.ls, local[0])

@@ -17,7 +17,7 @@ SCRATCH = {
     "cd": ("sbuf", [128, 16], "float32"),
     "ebase": ("sbuf", [128, 2], "float32"),
     "colg": ("sbuf", [128, 128], "bfloat16"),
-    "colp": ("sbuf", [128, 256], "bfloat16"),
+    "colp": ("sbuf", [128, 144], "bfloat16"),
     "n16": ("sbuf", [128, NP], "float32"),
     "jnum": ("sbuf", [128, 256], "bfloat16"),
     "vals": ("sbuf", [128, 256], "bfloat16"),
@@ -26,7 +26,7 @@ SCRATCH = {
     "ml": ("sbuf", [128, 128], "bfloat16"),
     "mr": ("sbuf", [128, 128], "bfloat16"),
     "mz": ("sbuf", [128, 144], "bfloat16"),
-    "me": ("sbuf", [128, 256], "bfloat16"),
+    "me": ("sbuf", [128, EL], "bfloat16"),
     "njl": ("sbuf", [128, 128], "bfloat16"),
     "jt": ("sbuf", [128, 16], "bfloat16"),
     "dm": ("sbuf", [128, 8], "bfloat16"),
@@ -34,35 +34,34 @@ SCRATCH = {
     "ct": ("sbuf", [4, 256], "bfloat16"),
     "cb": ("dram", [4, 128, 2], "bfloat16"),
     "rcnt": ("dram", [N, 128, 2], "bfloat16"),
-    "cnts": ("sbuf", [128, 16], "bfloat16"),
-    "mge": ("sbuf", [128, 128], "bfloat16"),
-    "mcum": ("sbuf", [128, 128], "bfloat16"),
+    "cnts": ("sbuf", [N, 4], "bfloat16"),
+    "mcum": ("sbuf", [N, 128], "bfloat16"),
+    "msel": ("sbuf", [N, 128], "bfloat16"),
     "mrf": ("sbuf", [128, 128], "float32"),
+    "mrh": ("sbuf", [128, 128], "float16"),
     "pcmp": ("sbuf", [128, NP], "float32"),
     "pbase": ("sbuf", [128, EL * NP], "float32"),
     "wgt": ("sbuf", [128, EL], "float32"),
-    "ff": ("sbuf", [128, EL * NP], "float32"),
+    "ff": ("sbuf", [128, EL * NP], "float16"),
     "ylist": ("sbuf", [128, EL * NP], "uint16"),
     "yt": ("sbuf", [128, EL * CAP], "bfloat16"),
     "pq": ("psum", [128, 512], "float32"),
     "pc": ("psum", [128, 512], "float32"),
-    "pcum": ("psum", [128, 512], "float32"),
-    "plr": ("psum", [128, 512], "float32"),
 }
 for _k in range(2):
     SCRATCH["oh%d" % _k] = ("sbuf", [128, 128], "bfloat16")
     SCRATCH["rc%d" % _k] = ("sbuf", [128, 136], "bfloat16")
     SCRATCH["v%d" % _k] = ("sbuf", [128, 128], "bfloat16")
     SCRATCH["rs%d" % _k] = ("sbuf", [128, 16], "bfloat16")
-    SCRATCH["rh%d" % _k] = ("sbuf", [128, 256], "bfloat16")
+    SCRATCH["rh%d" % _k] = ("sbuf", [128, EL], "bfloat16")
     SCRATCH["list%d" % _k] = ("sbuf", [128, 64], "uint16")
     SCRATCH["pp%d" % _k] = ("psum", [128, 512], "float32")
-    SCRATCH["pl%d" % _k] = ("psum", [128, 512], "float32")
 for _k in range(4):
     SCRATCH["sb%d" % _k] = ("sbuf", [128, BLK], "bfloat16")
 
-NEV = 64
-SEMAPHORES = ["exs", "xa", "xb", "xin", "cbs", "own", "cin", "cld", "arr", "ls", "ysa", "ysb"] + ["e%d" % i for i in range(NEV)]
+NEV = 80
+SEMAPHORES = (["exs", "xa", "xb", "xin", "cbs", "own", "cin", "cld", "arr", "rl", "ls", "ysa", "ysb"]
+              + ["e%d" % i for i in range(NEV)])
 
 
 def engines(mask):
@@ -74,15 +73,16 @@ def plan(r, cores, topo):
     order = [(r + i) % N for i in range(1, N)]
     direct = [d for d in order if topo.may_write(me, cores[d])]
     other = [d for d in order if not topo.may_write(me, cores[d])]
-    chip = topo.chip(me)
-    helpers = [c for c in range(128) if topo.chip(c) == chip and topo.die(c) != topo.die(me)
-               and all(topo.may_write(c, cores[d]) for d in other)]
-    return [(me, direct + [r]), (helpers[0], other[:2]), (helpers[1], other[2:])]
+    chip = [c for c in range(128) if topo.chip(c) == topo.chip(me) and c != me]
+    port = [c for c in chip if all(topo.may_write(c, cores[d]) for d in other)]
+    across = [c for c in port if topo.die(c) != topo.die(me)][0]
+    near = [c for c in port if topo.die(c) == topo.die(me)][0]
+    third = [c for c in chip if topo.die(c) != topo.die(me) and c != across and topo.may_write(c, cores[direct[0]])][0]
+    return [(me, direct + [r]), (across, other[:2]), (near, other[2:])], third
 
 
-def count_engines(w, r):
-    remote = [d for d in w[1] if d != r]
-    return 4 if len(remote) <= 2 else 2
+def cnt_engines(dests, r):
+    return 4 if len([d for d in dests if d != r]) <= 2 else 2
 
 
 def rank_program(g, core, T, topo):
@@ -91,17 +91,11 @@ def rank_program(g, core, T, topo):
     if not mine:
         return
     r = mine[0]
-    workers = plan(r, cores, topo)
-    me = [w for w in workers if w[0] == core]
-    if not me:
+    me = cores[r]
+    workers, third = plan(r, cores, topo)
+    dests = [ds for w, ds in workers if w == core]
+    if not dests and core != third:
         return
-    w = me[0]
-    dests = w[1]
-    is_rank = core == cores[r]
-    helpers = [h[0] for h in workers[1:]]
-    nd = len(dests)
-    K = nd // 2
-    TB = 1024 * K
     V, S, P, Y = g.vector, g.scalar, g.tensor, g.sync
     used = [0]
     local = [0]
@@ -110,6 +104,9 @@ def rank_program(g, core, T, topo):
     def group():
         used[0] += 1
         return {"sem": T.sem["e%d" % (used[0] - 1)], "n": 0, "key": used[0]}
+
+    def named(name, n):
+        return {"sem": T.sem[name], "n": n, "key": name}
 
     def add(grp, inst):
         inst.then_inc(grp["sem"], 1)
@@ -132,46 +129,58 @@ def rank_program(g, core, T, topo):
         g.remote_dma(out, in_, rsem, T.sem.ls, pid, rid, mask)
         local[0] += len(engines(mask))
 
-    def send_fused(parts, rsem):
+    def send_fused(parts):
         tr = []
-        for dst, out, in_, eng in parts:
+        for dst, out, in_, eng, rsem in parts:
             rid, pid, _s = topo.addr(dst)
             tr.append(RemoteDMATransfer(dst_ids=[DstId(rid=rid, pnc=pid)], dma_engine_mask=sum(eng), remote_sem=rsem,
                                         src=in_, dst=out))
             local[0] += len(eng)
         g.remote_dma_fused(tr, local_sem=T.sem.ls)
 
+    landing = T.recv[:, r * BLK:(r + 1) * BLK]
+    if core == third:
+        dst = cores[workers[0][1][0]]
+        g.wait_ge(T.sem.rl, len(engines(topo.mask(me, core))))
+        send(dst, landing, T.sb0[:, :], T.sem.arr, topo.mask(core, dst))
+        g.wait_ge(T.sem.ls, local[0])
+        return
+    dests = dests[0]
+    nd = len(dests)
+    K = nd // 2
+    TB = 1024 * K
+    is_rank = core == me
+    helpers = [w for w, _ds in workers[1:]]
+
     half = TOK // 2
-    onchip = engines(topo.mask(core, helpers[0])) if is_rank else []
     if is_rank:
         for q in range(4):
             Y.dma_start(T.exi[16 * q:16 * q + 16, :], T.ex[:, :]).then_inc(T.sem.exs, 16)
             S.dma_start(T.exi[64 + 16 * q:80 + 16 * q, :], T.ex[:, :]).then_inc(T.sem.exs, 16)
         Y.dma_start(T.xs[:, 0:half], T.x[:, 0:half]).then_inc(T.sem.xa, 16)
         S.dma_start(T.xs[:, half:TOK], T.x[:, half:TOK]).then_inc(T.sem.xb, 16)
-        exw = {"sem": T.sem.exs, "n": 128, "key": "ex"}
-        xw = [{"sem": T.sem.xa, "n": 16, "key": "xa"}, {"sem": T.sem.xb, "n": 16, "key": "xb"}]
+        exw = named("exs", 128)
+        xw = [named("xa", 16), named("xb", 16)]
     else:
-        exw = {"sem": T.sem.exs, "n": 8, "key": "ex"}
-        first = core == helpers[0]
-        nx = len(engines(topo.mask(cores[r], core)))
-        xw = [{"sem": T.sem.xin, "n": nx * (2 if first else 1), "key": "xin"}]
+        nx = len(engines(topo.mask(me, core)))
+        exw = named("exs", nx // 2)
+        xw = [named("xin", nx * (2 if core == helpers[0] else 1))]
 
     it_row = one(g.iota(T.ci[:, 0:1], [[0, 1]], 0, 1))
-    it_cp = one(g.iota(T.colp[:, :], [[0, 16], [1, 16]], 0, 0, allow_small_or_imprecise_dtypes=True))
+    it_cp = one(g.iota(T.colp[:, :], [[0, 9], [1, 16]], 0, 0, allow_small_or_imprecise_dtypes=True))
     it_cg = one(g.iota(T.colg[:, :], [[1, 8], [0, 16]], 0, 0, allow_small_or_imprecise_dtypes=True))
     it_jn = group()
     add(it_jn, g.iota(T.n16[:, :], [[16, NP]], 0, 0, allow_small_or_imprecise_dtypes=True))
     add(it_jn, g.iota(T.jnum[:, :], [[1, 16], [16, 16]], 0, 0, allow_small_or_imprecise_dtypes=True))
     if is_rank:
+        eng = engines(topo.mask(me, helpers[0]))
         wait("g", g, exw)
-        send_fused([(helpers[i], T.exi[:, :], T.exi[:, :], onchip[8 * i:8 * i + 8]) for i in range(2)], T.sem.exs)
+        send_fused([(c, T.exi[:, :], T.exi[:, :], eng[8 * i:8 * i + 8], T.sem.exs) for i, c in enumerate(helpers)])
         wait("g", g, xw[0])
-        send(helpers[0], T.xs[:, 0:half], T.xs[:, 0:half], T.sem.xin, sum(onchip))
+        send(helpers[0], T.xs[:, 0:half], T.xs[:, 0:half], T.sem.xin, sum(eng))
         wait("g", g, xw[1])
-        send(helpers[0], T.xs[:, half:TOK], T.xs[:, half:TOK], T.sem.xin, sum(onchip))
-        send(helpers[1], T.xs[:, :], T.xs[:, :], T.sem.xin, sum(onchip))
-        it_pb = one(g.iota(T.pbase[0:16, :], [[CAPP, EL], [16, NP]], 0, 1, allow_small_or_imprecise_dtypes=True))
+        send(helpers[0], T.xs[:, half:TOK], T.xs[:, half:TOK], T.sem.xin, sum(eng))
+        send(helpers[1], T.xs[:, :], T.xs[:, :], T.sem.xin, sum(eng))
 
     rg, rp, g4 = T.cf[:, 1:2], T.cf[:, 2:3], T.cf[:, 3:4]
 
@@ -179,81 +188,116 @@ def rank_program(g, core, T, topo):
         return T.cd[:, i:i + 1]
     m0 = group()
     for k in range(K):
-        add(m0, V.memset(T["rc%d" % k][:, 0:8], 0.0))
         add(m0, V.memset(T.ebase[0:64, k:k + 1], float(EL * dests[2 * k])))
         add(m0, V.memset(T.ebase[64:128, k:k + 1], float(EL * dests[2 * k + 1])))
-    add(m0, V.memset(T.dm[:, 0:nd * K], 0.0))
-    wz = group()
-    vz = 512 if is_rank else TB
-    add(wz, V.memset(T.win[:, 0:vz], 0.0))
-    for c in range(vz, TB, 256):
-        wait("S", S, it_cp)
-        add(wz, S.activation(T.win[:, c:c + 256], T.colp[:, :], F.Copy, scale=0.0))
     wait("V", V, it_row)
     s1 = group()
     add(s1, V.tensor_scalar(T.ci[:, 1:2], T.ci[:, 0:1], 4, None, A.arith_shift_right))
     add(s1, V.tensor_scalar(T.ci[:, 2:3], T.ci[:, 0:1], 15, None, A.bitwise_and))
     add(s1, V.tensor_scalar(T.ci[:, 3:4], T.ci[:, 0:1], 4, 3, A.arith_shift_right, A.bitwise_and))
+    z0 = group()
+    for k in range(K):
+        add(z0, V.memset(T["rc%d" % k][:, 0:8], 0.0))
+    add(z0, V.memset(T.dm[:, 0:nd * K], 0.0))
+    add(z0, V.memset(T.ct[:, :], 0.0))
     wait("V", V, s1)
     s2 = one(V.tensor_copy(T.cf[:, :], T.ci[:, :]))
+    wz = group()
+    vz = 512 if is_rank else TB
+    add(wz, V.memset(T.win[:, 0:vz], 0.0))
+    for c in range(vz, TB, 128):
+        wait("S", S, it_cp)
+        add(wz, S.activation(T.win[:, c:c + 128], T.colp[:, 0:128], F.Copy, scale=0.0))
     wait("V", V, s2, m0)
     s3 = group()
-    for k in range(K):
-        add(s3, V.tensor_scalar(cd(6 + k), T.ebase[:, k:k + 1], g4, None, A.add))
+    add(s3, V.tensor_scalar(T.cd[:, 8:8 + K], T.ebase[:, 0:K], g4, None, A.add))
     add(s3, V.tensor_scalar(cd(0), rp, -16.0, None, A.mult))
-    s5 = group()
-    add(s5, V.tensor_scalar(cd(1), rp, 0.0, None, A.is_equal))
-    add(s5, V.tensor_scalar(cd(8), rp, 0.0, None, A.is_gt))
-    add(s5, V.tensor_scalar(cd(2), rp, 1.0, rg, A.is_equal, A.mult))
-    for k in range(K):
-        add(s5, V.tensor_scalar(cd(4 + k), rg, 128.0, float(1024 * k - TB), A.mult, A.add))
+    wait("V", V, it_cp)
+    gt = one(V.tensor_scalar(T.mgt[:, :], T.colp[:, 0:128], rp, None, A.is_gt))
+    mr = one(V.tensor_scalar(T.mr[:, :], T.colp[:, 0:128], rp, None, A.is_equal))
+    me4 = one(V.tensor_scalar(T.me[:, :], T.colp[:, 0:EL], g4, None, A.is_equal))
+    wait("V", V, it_cg)
+    mb = one(V.tensor_scalar(T.mb[:, :], T.colg[:, :], rg, None, A.is_equal))
+    wait("V", V, s3)
+    njl = one(V.tensor_scalar(T.njl[:, :], T.colp[:, 0:128], -1.0, cd(0), A.mult, A.add))
+    wait("V", V, z0)
     dmg = group()
     for k in range(K):
         add(dmg, V.memset(T.dm[0:64, nd * k + 2 * k:nd * k + 2 * k + 1], 1.0))
         add(dmg, V.memset(T.dm[64:128, nd * k + 2 * k + 1:nd * k + 2 * k + 2], 1.0))
-    wait("V", V, it_cp)
-    gt = one(V.tensor_scalar(T.mgt[:, :], T.colp[:, 0:128], rp, None, A.is_gt))
-    mr = one(V.tensor_scalar(T.mr[:, :], T.colp[:, 0:128], rp, None, A.is_equal))
-    wait("V", V, s3)
-    njl = one(V.tensor_scalar(T.njl[:, :], T.colp[:, 0:128], -1.0, cd(0), A.mult, A.add))
-    me = one(V.tensor_scalar(T.me[:, :], T.colp[:, :], g4, None, A.is_equal))
-    wait("V", V, it_cg)
-    mb = one(V.tensor_scalar(T.mb[:, :], T.colg[:, :], rg, None, A.is_equal))
     wait("V", V, mb, gt)
     ml = one(V.tensor_tensor(T.ml[:, :], T.mgt[:, :], T.mb[:, :], A.mult))
 
+    s5, jt, kc = group(), group(), {}
+
+    def consts_a():
+        add(s5, V.tensor_scalar(cd(4), rp, 0.0, None, A.is_equal))
+        add(s5, V.tensor_scalar(cd(5), rp, 0.0, None, A.is_gt))
+        add(s5, V.tensor_scalar(cd(2), rp, 1.0, rg, A.is_equal, A.mult))
+        for k in range(K):
+            add(s5, V.tensor_scalar(cd(12 + k), rg, 128.0, float(1024 * k - TB), A.mult, A.add))
+        wait("V", V, it_jn, mr)
+        add(jt, V.tensor_scalar(T.jt[:, :], T.n16[:, 0:16], rp, None, A.add))
+
+    def consts_b():
+        wait("V", V, s5)
+        for k in range(K):
+            add(jt, V.tensor_scalar(T["rs%d" % k][:, :], T.colp[:, 0:16], rp, cd(12 + k), A.is_equal, A.mult))
+
+    def consts_c():
+        wt = one(V.tensor_scalar(cd(3), cd(2), 256.0, cd(4), A.mult, A.add))
+        kc["va"] = one(V.tensor_scalar(T.vals[:, :], T.jnum[:, :], cd(4), cd(5), A.mult, A.add))
+        wait("V", V, wt)
+        kc["mz"] = one(V.tensor_scalar(T.mz[:, :], T.colp[:, 0:144], 15.0, cd(3), A.is_equal, A.mult))
+    if not is_rank:
+        consts_a()
+        consts_b()
+        consts_c()
+
     wait("V", V, exw)
-    oh, sc, pl = [], [], []
+    oh, sc, pl, mul = [], [], [], []
+
+    def masked(k):
+        wait("V", V, pl[k])
+        mul.append(one(V.tensor_tensor(T["v%d" % k][:, :], T["pp%d" % k][:, 0:128], T["oh%d" % k][:, :], A.mult)))
+
     for k in range(K):
-        oh.append(one(V.tensor_scalar(T["oh%d" % k][:, :], T.exi[:, :], cd(6 + k), None, A.is_equal)))
+        oh.append(one(V.tensor_scalar(T["oh%d" % k][:, :], T.exi[:, :], cd(8 + k), None, A.is_equal)))
     for k in range(K):
-        wait("V", V, oh[k])
         o = T["oh%d" % k]
+        wait("V", V, oh[k])
         sc.append(one(V.tensor_tensor_scan(T["rc%d" % k][:, 8:136], o[:, :], o[:, :], 0.0, A.add, A.max)))
     wait("P", P, mr, njl)
     for k in range(K):
         P.matmul(T["pp%d" % k][:, 0:128], T.mr[0:16, :], T.njl[0:16, :], True, False)
-    wait("P", P, mb, ml, m0)
+    wait("P", P, mb, ml, z0)
     for k in range(K):
         o, c, pp = T["oh%d" % k], T["rc%d" % k], T["pp%d" % k]
         wait("P", P, oh[k])
         P.matmul(pp[:, 0:128], T.ml[:, :], o[:, :], False, False)
         wait("P", P, sc[k])
         pl.append(one(P.matmul(pp[:, 0:128], T.mb[:, :], c[:, 7:135], False, True)))
-    wait("V", V, it_jn, mr, s5)
-    jt = group()
-    add(jt, V.tensor_scalar(T.jt[:, :], T.n16[:, 0:16], rp, None, A.add))
-    for k in range(K):
-        add(jt, V.tensor_scalar(T["rs%d" % k][:, :], T.colp[:, 0:16], rp, cd(4 + k), A.is_equal, A.mult))
-    wait("V", V, me)
     rh = group()
+    wait("V", V, me4)
     for k in range(K):
         wait("V", V, sc[k])
         add(rh, V.tensor_scalar(T["rh%d" % k][:, :], T.me[:, :], T["rc%d" % k][:, 135:136], None, A.mult))
-    mul = []
+    wait("P", P, dmg, rh)
     for k in range(K):
-        wait("V", V, pl[k])
-        mul.append(one(V.tensor_tensor(T["v%d" % k][:, :], T["pp%d" % k][:, 0:128], T["oh%d" % k][:, :], A.mult)))
+        inst = P.matmul(T.pc[0:nd, 0:EL], T.dm[:, nd * k:nd * k + nd], T["rh%d" % k][:, :], k == 0, k == K - 1)
+    pc = one(inst)
+    wait("S", S, pc, z0)
+    ctd = one(S.activation(T.ct[0:nd, 0:EL], T.pc[0:nd, 0:EL], F.Copy))
+    wait("Y", Y, ctd)
+    Y.dma_start(T.cb[0:nd], T.ct[0:nd, :]).then_inc(T.sem.cbs, 16)
+    if is_rank:
+        Y.dma_start(T.rcnt[r], T.ct[nd - 1:nd, :]).then_inc(T.sem.own, 16)
+        consts_a()
+    masked(0)
+    if is_rank:
+        consts_b()
+    for k in range(1, K):
+        masked(k)
     wait("P", P, jt)
     P.matmul(T.pq[:, 0:16], T.mr[0:16, :], T.jt[0:16, :], True, False)
     for k in range(K):
@@ -262,102 +306,102 @@ def rank_program(g, core, T, topo):
         wait("P", P, mul[k])
         inst = P.matmul(T.pq[:, 0:16], T["v%d" % k][:, :], T.mr[:, 0:16], False, k == K - 1)
     qd = one(inst)
-    wt = one(V.tensor_scalar(cd(3), cd(2), 256.0, cd(1), A.mult, A.add))
-    va = one(V.tensor_scalar(T.vals[:, :], T.jnum[:, :], cd(1), cd(8), A.mult, A.add))
-    wait("V", V, wt)
-    mz = one(V.tensor_scalar(T.mz[:, :], T.colp[:, 0:144], 15.0, cd(3), A.is_equal, A.mult))
+    if is_rank:
+        consts_c()
     wait("V", V, qd)
     of = one(V.tensor_scalar(T.off[:, :], T.pq[:, 0:16], float(TB), None, A.add))
-    wait("V", V, of, va, wz)
+    wait("V", V, of, kc["va"], wz)
     scat = one(V.tensor_copy(T.win[:, 0:TB + 256].indirect(T.off[:, 0:16]), T.vals[:, :]))
-    wait("P", P, dmg, rh)
-    for k in range(K):
-        inst = P.matmul(T.pc[0:nd, 0:256], T.dm[:, nd * k:nd * k + nd], T["rh%d" % k][:, :], k == 0, k == K - 1)
-    pc = one(inst)
-    wait("S", S, pc)
-    ctd = one(S.activation(T.ct[0:nd, :], T.pc[0:nd, 0:256], F.Copy))
-    remote = [d for d in dests if d != r]
-    nr = len(remote)
-    wait("Y", Y, ctd)
-    Y.dma_start(T.cb[0:nr], T.ct[0:nr, :]).then_inc(T.sem.cbs, 16)
-    if is_rank:
-        Y.dma_start(T.rcnt[r], T.ct[nr:nd, :]).then_inc(T.sem.own, 16)
-    wait("P", P, scat, mz)
+    wait("P", P, scat, kc["mz"])
     ll = []
     for k in range(K):
         for m in range(16):
-            inst = P.matmul(T["pl%d" % k][:, 0:64], T.mz[:, 15 - m:143 - m], T.win[:, 1024 * k + m:1024 * (k + 1):16],
+            inst = P.matmul(T["pp%d" % k][:, 0:64], T.mz[:, 15 - m:143 - m], T.win[:, 1024 * k + m:1024 * (k + 1):16],
                             m == 0, m == 15)
         ll.append(one(inst))
     blk = []
     for k in range(K):
         wait("V", V, ll[k])
-        lk = one(V.tensor_copy(T["list%d" % k][:, :], T["pl%d" % k][:, 0:64]))
+        lk = one(V.tensor_copy(T["list%d" % k][:, :], T["pp%d" % k][:, 0:64]))
         wait("V", V, lk, *xw)
         wait("S", S, lk, *xw)
-        for h in range(2):
-            di = 2 * k + h
-            out = T.recv[:, r * BLK:(r + 1) * BLK] if dests[di] == r else T["sb%d" % di][:, :]
-            src = T.xs[:, :].indirect(T["list%d" % k][:, 32 * h:32 * h + 32])
-            blk.append(one(V.tensor_copy(out, src) if h == 0 else S.activation(out, src, F.Copy)))
-    ne = count_engines(w, r)
-    wait("g", g, {"sem": T.sem.cbs, "n": 16, "key": "cbs"})
-    parts = []
-    for i, d in enumerate(remote):
-        eng = engines(topo.mask(core, cores[d]))
-        parts.append((cores[d], T.rcnt[r], T.cb[i], eng[ne * i:ne * i + ne]))
-    send_fused(parts, T.sem.cin)
-    for i, d in enumerate(remote):
-        wait("g", g, blk[i])
-        send(cores[d], T.recv[:, r * BLK:(r + 1) * BLK], T["sb%d" % i][:, :], T.sem.arr, topo.mask(core, cores[d]))
+        for i in (2 * k, 2 * k + 1):
+            buf, b0 = (T.recv, r * BLK) if dests[i] == r else (T["sb%d" % i], 0)
+            a = 32 * (i - 2 * k)
+            two = group()
+            for q in range(2):
+                src = T.xs[:, :].indirect(T["list%d" % k][:, a + 16 * q:a + 16 * q + 16])
+                dst = buf[:, b0 + 256 * q:b0 + 256 * q + 256]
+                add(two, V.tensor_copy(dst, src) if q == 0 else S.activation(dst, src, F.Copy))
+            blk.append(two)
+    wait("g", g, named("cbs", 16))
+    remote = [i for i in range(nd) if dests[i] != r]
+    ne = cnt_engines(dests, r)
+    send_fused([(cores[dests[i]], T.rcnt[r], T.cb[i], engines(topo.mask(core, cores[dests[i]]))[ne * i:ne * i + ne], T.sem.cin)
+                for i in remote])
     if is_rank:
-        zz = one(V.memset(T.recv[:, ZERO:ZERO + NZ], 0.0))
-        ge = one(V.tensor_scalar(T.mge[:, :], T.colg[:, :], rg, None, A.is_ge))
-        mrf = one(V.tensor_copy(T.mrf[:, :], T.mr[:, :]))
-        pcm = one(V.tensor_scalar(T.pcmp[:, :], T.n16[:, :], rp, None, A.add))
-        wait("V", V, ge)
-        cm = one(V.tensor_tensor(T.mcum[:, :], T.mge[:, :], T.mr[:, :], A.mult))
-        ncin = narr = 0
-        for q in range(N):
-            if q == r:
-                continue
-            for v in plan(q, cores, topo):
-                if r in v[1]:
-                    ncin += count_engines(v, q)
-                    narr += len(engines(topo.mask(v[0], core)))
-        Y.wait_ge(T.sem.own, 16)
-        Y.wait_ge(T.sem.cin, ncin)
-        Y.dma_start(T.cnts[:, :], T.rcnt[:]).then_inc(T.sem.cld, 16)
-        cl = {"sem": T.sem.cld, "n": 16, "key": "cld"}
-        wait("P", P, it_pb, mrf)
-        P.matmul(T.plr[:, 0:EL * NP], T.mrf[0:16, :], T.pbase[0:16, :], True, False)
-        wait("P", P, cl, cm)
-        cum = one(P.matmul(T.pcum[:, 0:EL], T.mcum[:, :], T.cnts[:, 0:EL], True, True))
-        wait("V", V, cl)
-        wg = one(V.tensor_scalar(T.wgt[:, :], T.cnts[:, 0:EL], -1.0, float(BLK), A.mult, A.add))
-        wait("V", V, cum, wg, pcm)
-        ff = group()
-        for e in range(EL):
-            add(ff, V.tensor_scalar(T.ff[:, NP * e:NP * e + NP], T.pcmp[:, :], T.pcum[:, e:e + 1], T.wgt[:, e:e + 1],
-                                    A.is_ge, A.mult))
-        wait("P", P, ff)
-        lr = one(P.matmul(T.plr[:, 0:EL * NP], T.mrf[:, :], T.ff[:, :], False, True))
-        wait("V", V, lr)
-        yl = one(V.tensor_copy(T.ylist[:, :], T.plr[:, 0:EL * NP]))
-        ar = {"sem": T.sem.arr, "n": narr, "key": "arr"}
-        wait("V", V, yl, ar, zz, blk[nd - 1])
-        wait("S", S, yl, ar, zz, blk[nd - 1])
-        yo = {}
-        for i in range(2):
-            for q, e in ((0, i), (1, 2 + i)):
-                src = T.recv[:, :].indirect(T.ylist[:, NP * e:NP * e + NP])
-                out = T.yt[:, CAP * e:CAP * e + CAP]
-                yo[e] = one(V.tensor_copy(out, src) if q == 0 else S.activation(out, src, F.Copy))
-        for e in (0, 2, 1):
-            wait("Y", Y, yo[e])
-            Y.dma_start(T.y[:, CAP * e:CAP * e + CAP], T.yt[:, CAP * e:CAP * e + CAP]).then_inc(T.sem.ysa, 16)
-        wait("S", S, yo[3])
-        S.dma_start(T.y[:, 3 * CAP:4 * CAP], T.yt[:, 3 * CAP:4 * CAP]).then_inc(T.sem.ysb, 16)
-        Y.wait_ge(T.sem.ysa, 48)
-        S.wait_ge(T.sem.ysb, 16)
+        it_pb = one(g.iota(T.pbase[0:16, :], [[CAPP, EL], [16, NP]], 0, 1, allow_small_or_imprecise_dtypes=True))
+    for i in remote:
+        wait("g", g, blk[i])
+        if is_rank and i == 0:
+            send(third, T.sb0[:, :], T.sb0[:, :], T.sem.rl, topo.mask(core, third))
+        else:
+            send(cores[dests[i]], landing, T["sb%d" % i][:, :], T.sem.arr, topo.mask(core, cores[dests[i]]))
+    if not is_rank:
+        g.wait_ge(T.sem.ls, local[0])
+        return
+
+    zz = one(V.memset(T.recv[:, ZERO:ZERO + NZ], 0.0))
+    rq = T.cf[0:N, 0:1]
+    cm = group()
+    add(cm, V.tensor_scalar(T.mcum[:, :], T.colg[0:N, :], rq, None, A.is_ge))
+    add(cm, V.tensor_scalar(T.msel[:, :], T.colg[0:N, :], rq, None, A.is_equal))
+    mrf = group()
+    add(mrf, V.tensor_copy(T.mrf[:, :], T.mr[:, :]))
+    add(mrf, V.tensor_copy(T.mrh[:, :], T.mr[:, :]))
+    pcm = one(V.tensor_scalar(T.pcmp[:, :], T.n16[:, :], rp, None, A.add))
+    ncin = narr = 0
+    for q in range(N):
+        if q == r:
+            continue
+        ws, th = plan(q, cores, topo)
+        for w, ds in ws:
+            if r in ds:
+                ncin += cnt_engines(ds, q)
+                narr += len(engines(topo.mask(th if w == cores[q] and ds[0] == r else w, me)))
+    Y.wait_ge(T.sem.own, 16)
+    Y.wait_ge(T.sem.cin, ncin)
+    Y.dma_start(T.cnts[:, :], T.rcnt[:, 0:2, :]).then_inc(T.sem.cld, 16)
+    wait("P", P, it_pb, mrf, of)
+    P.matmul(T.pq[:, 0:EL * NP], T.mrf[0:16, :], T.pbase[0:16, :], True, False)
+    wait("P", P, named("cld", 16), cm)
+    P.matmul(T.pc[:, 8:8 + EL], T.msel[:, :], T.cnts[:, :], True, True)
+    cum = one(P.matmul(T.pc[:, 0:EL], T.mcum[:, :], T.cnts[:, :], True, True))
+    wait("V", V, cum)
+    wg = one(V.tensor_scalar(T.wgt[:, :], T.pc[:, 8:8 + EL], -1.0, float(BLK), A.mult, A.add))
+    wait("V", V, wg, pcm)
+    ff = group()
+    for e in range(EL):
+        add(ff, V.tensor_scalar(T.ff[:, NP * e:NP * e + NP], T.pcmp[:, :], T.pc[:, e:e + 1], T.wgt[:, e:e + 1],
+                                A.is_ge, A.mult))
+    wait("P", P, ff)
+    lr = one(P.matmul(T.pq[:, 0:EL * NP], T.mrh[:, :], T.ff[:, :], False, True))
+    wait("V", V, lr)
+    yl = one(V.tensor_copy(T.ylist[:, :], T.pq[:, 0:EL * NP]))
+    ar = named("arr", narr)
+    wait("V", V, yl, ar, zz, blk[-1])
+    wait("S", S, yl, ar, zz, blk[-1])
+    yo = {}
+    for i in range(2):
+        for q, e in ((0, i), (1, 2 + i)):
+            src = T.recv[:, :].indirect(T.ylist[:, NP * e:NP * e + NP])
+            out = T.yt[:, CAP * e:CAP * e + CAP]
+            yo[e] = one(V.tensor_copy(out, src) if q == 0 else S.activation(out, src, F.Copy))
+    for e in (0, 2, 1):
+        wait("Y", Y, yo[e])
+        Y.dma_start(T.y[:, CAP * e:CAP * e + CAP], T.yt[:, CAP * e:CAP * e + CAP]).then_inc(T.sem.ysa, 16)
+    wait("S", S, yo[3])
+    S.dma_start(T.y[:, 3 * CAP:4 * CAP], T.yt[:, 3 * CAP:4 * CAP]).then_inc(T.sem.ysb, 16)
+    Y.wait_ge(T.sem.ysa, 48)
+    S.wait_ge(T.sem.ysb, 16)
     g.wait_ge(T.sem.ls, local[0])

from concourse.bass import DstId, RemoteDMATransfer
from concourse.mybir import AluOpType as A, ActivationFunctionType as F

N, TOK, EL, CAP, CAPP = 8, 2048, 4, 480, 128
BLK = EL * CAPP
ZERO = N * BLK
NZ = (EL - 1) * CAPP + CAP
NP = CAP // 16

SCRATCH = {
    "exi": ("sbuf", [128, 128], "int32"),
    "xs": ("sbuf", [128, TOK], "bfloat16"),
    "recv": ("sbuf", [128, ZERO + NZ], "bfloat16"),
    "win": ("sbuf", [128, 2048 + 256], "bfloat16"),
    "ci": ("sbuf", [128, 4], "int32"),
    "cf": ("sbuf", [128, 4], "float32"),
    "cd": ("sbuf", [128, 16], "float32"),
    "ebase": ("sbuf", [128, 2], "float32"),
    "colg": ("sbuf", [128, 128], "bfloat16"),
    "colp": ("sbuf", [128, 144], "bfloat16"),
    "n16": ("sbuf", [128, NP], "float32"),
    "jnum": ("sbuf", [128, 256], "bfloat16"),
    "vals": ("sbuf", [128, 256], "bfloat16"),
    "mb": ("sbuf", [128, 128], "bfloat16"),
    "mgt": ("sbuf", [128, 128], "bfloat16"),
    "ml": ("sbuf", [128, 128], "bfloat16"),
    "mr": ("sbuf", [128, 128], "bfloat16"),
    "mz": ("sbuf", [128, 144], "bfloat16"),
    "me": ("sbuf", [128, EL], "bfloat16"),
    "njl": ("sbuf", [128, 128], "bfloat16"),
    "jt": ("sbuf", [128, 16], "bfloat16"),
    "dm": ("sbuf", [128, 8], "bfloat16"),
    "off": ("sbuf", [128, 16], "uint16"),
    "ct": ("sbuf", [4, 256], "bfloat16"),
    "cb": ("dram", [4, 128, 2], "bfloat16"),
    "rcnt": ("dram", [N, 128, 2], "bfloat16"),
    "cnts": ("sbuf", [N, 4], "bfloat16"),
    "mcum": ("sbuf", [N, 128], "bfloat16"),
    "msel": ("sbuf", [N, 128], "bfloat16"),
    "mrf": ("sbuf", [128, 128], "float32"),
    "mrh": ("sbuf", [128, 128], "float16"),
    "pcmp": ("sbuf", [128, NP], "float32"),
    "pbase": ("sbuf", [128, EL * NP], "float32"),
    "wgt": ("sbuf", [128, EL], "float32"),
    "ff": ("sbuf", [128, EL * NP], "float16"),
    "ylist": ("sbuf", [128, EL * NP], "uint16"),
    "yt": ("sbuf", [128, EL * CAP], "bfloat16"),
    "pq": ("psum", [128, 512], "float32"),
    "pc": ("psum", [128, 512], "float32"),
}
for _k in range(2):
    SCRATCH["oh%d" % _k] = ("sbuf", [128, 128], "bfloat16")
    SCRATCH["rc%d" % _k] = ("sbuf", [128, 136], "bfloat16")
    SCRATCH["v%d" % _k] = ("sbuf", [128, 128], "bfloat16")
    SCRATCH["rs%d" % _k] = ("sbuf", [128, 16], "bfloat16")
    SCRATCH["rh%d" % _k] = ("sbuf", [128, EL], "bfloat16")
    SCRATCH["list%d" % _k] = ("sbuf", [128, 64], "uint16")
    SCRATCH["pp%d" % _k] = ("psum", [128, 512], "float32")
for _k in range(4):
    SCRATCH["sb%d" % _k] = ("sbuf", [128, BLK], "bfloat16")

NEV = 80
SEMAPHORES = (["exs", "xa", "xb", "xin", "cbs", "own", "cin", "cld", "arr", "rl", "ls", "ysa", "ysb"]
              + ["e%d" % i for i in range(NEV)])


def engines(mask):
    return [1 << b for b in range(mask.bit_length()) if (mask >> b) & 1]


def plan(r, cores, topo):
    me = cores[r]
    order = [(r + i) % N for i in range(1, N)]
    direct = [d for d in order if topo.may_write(me, cores[d])]
    other = [d for d in order if not topo.may_write(me, cores[d])]
    chip = [c for c in range(128) if topo.chip(c) == topo.chip(me) and c != me]
    port = [c for c in chip if all(topo.may_write(c, cores[d]) for d in other)]
    across = [c for c in port if topo.die(c) != topo.die(me)][0]
    near = [c for c in port if topo.die(c) == topo.die(me)][0]
    third = [c for c in chip if topo.die(c) != topo.die(me) and c != across and topo.may_write(c, cores[direct[0]])][0]
    return [(me, direct + [r]), (across, other[:2]), (near, other[2:])], third


def cnt_engines(dests, r):
    return 4 if len([d for d in dests if d != r]) <= 2 else 2


def rank_program(g, core, T, topo):
    cores = list(T.cores)
    mine = [q for q in range(N) if topo.chip(cores[q]) == topo.chip(core)]
    if not mine:
        return
    r = mine[0]
    me = cores[r]
    workers, third = plan(r, cores, topo)
    dests = [ds for w, ds in workers if w == core]
    if not dests and core != third:
        return
    V, S, P, Y = g.vector, g.scalar, g.tensor, g.sync
    used = [0]
    local = [0]
    seen = {}

    def group():
        used[0] += 1
        return {"sem": T.sem["e%d" % (used[0] - 1)], "n": 0, "key": used[0]}

    def named(name, n):
        return {"sem": T.sem[name], "n": n, "key": name}

    def add(grp, inst):
        inst.then_inc(grp["sem"], 1)
        grp["n"] += 1

    def one(inst):
        grp = group()
        add(grp, inst)
        return grp

    def wait(name, q, *grps):
        for grp in grps:
            if (name, grp["key"]) in seen:
                continue
            seen[(name, grp["key"])] = True
            q.wait_ge(grp["sem"], grp["n"])

    def send(dst, out, in_, rsem, mask):
        rid, pid, _s = topo.addr(dst)
        g.remote_dma(out, in_, rsem, T.sem.ls, pid, rid, mask)
        local[0] += len(engines(mask))

    def send_fused(parts):
        tr = []
        for dst, out, in_, eng, rsem in parts:
            rid, pid, _s = topo.addr(dst)
            tr.append(RemoteDMATransfer(dst_ids=[DstId(rid=rid, pnc=pid)], dma_engine_mask=sum(eng), remote_sem=rsem,
                                        src=in_, dst=out))
            local[0] += len(eng)
        g.remote_dma_fused(tr, local_sem=T.sem.ls)

    landing = T.recv[:, r * BLK:(r + 1) * BLK]
    if core == third:
        dst = cores[workers[0][1][0]]
        g.wait_ge(T.sem.rl, len(engines(topo.mask(me, core))))
        send(dst, landing, T.sb0[:, :], T.sem.arr, topo.mask(core, dst))
        g.wait_ge(T.sem.ls, local[0])
        return
    dests = dests[0]
    nd = len(dests)
    K = nd // 2
    TB = 1024 * K
    is_rank = core == me
    helpers = [w for w, _ds in workers[1:]]

    half = TOK // 2
    if is_rank:
        for q in range(4):
            Y.dma_start(T.exi[16 * q:16 * q + 16, :], T.ex[:, :]).then_inc(T.sem.exs, 16)
            S.dma_start(T.exi[64 + 16 * q:80 + 16 * q, :], T.ex[:, :]).then_inc(T.sem.exs, 16)
        Y.dma_start(T.xs[:, 0:half], T.x[:, 0:half]).then_inc(T.sem.xa, 16)
        S.dma_start(T.xs[:, half:TOK], T.x[:, half:TOK]).then_inc(T.sem.xb, 16)
        exw = named("exs", 128)
        xw = [named("xa", 16), named("xb", 16)]
    else:
        nx = len(engines(topo.mask(me, core)))
        exw = named("exs", nx // 2)
        xw = [named("xin", nx * (2 if core == helpers[0] else 1))]

    it_row = one(g.iota(T.ci[:, 0:1], [[0, 1]], 0, 1))
    it_cp = one(g.iota(T.colp[:, :], [[0, 9], [1, 16]], 0, 0, allow_small_or_imprecise_dtypes=True))
    it_cg = one(g.iota(T.colg[:, :], [[1, 8], [0, 16]], 0, 0, allow_small_or_imprecise_dtypes=True))
    it_jn = group()
    add(it_jn, g.iota(T.n16[:, :], [[16, NP]], 0, 0, allow_small_or_imprecise_dtypes=True))
    add(it_jn, g.iota(T.jnum[:, :], [[1, 16], [16, 16]], 0, 0, allow_small_or_imprecise_dtypes=True))
    if is_rank:
        eng = engines(topo.mask(me, helpers[0]))
        wait("g", g, exw)
        send_fused([(c, T.exi[:, :], T.exi[:, :], eng[8 * i:8 * i + 8], T.sem.exs) for i, c in enumerate(helpers)])
        wait("g", g, xw[0])
        send(helpers[0], T.xs[:, 0:half], T.xs[:, 0:half], T.sem.xin, sum(eng))
        wait("g", g, xw[1])
        send(helpers[0], T.xs[:, half:TOK], T.xs[:, half:TOK], T.sem.xin, sum(eng))
        send(helpers[1], T.xs[:, :], T.xs[:, :], T.sem.xin, sum(eng))

    rg, rp, g4 = T.cf[:, 1:2], T.cf[:, 2:3], T.cf[:, 3:4]

    def cd(i):
        return T.cd[:, i:i + 1]
    m0 = group()
    for k in range(K):
        add(m0, V.memset(T.ebase[0:64, k:k + 1], float(EL * dests[2 * k])))
        add(m0, V.memset(T.ebase[64:128, k:k + 1], float(EL * dests[2 * k + 1])))
    wait("V", V, it_row)
    s1 = group()
    add(s1, V.tensor_scalar(T.ci[:, 1:2], T.ci[:, 0:1], 4, None, A.arith_shift_right))
    add(s1, V.tensor_scalar(T.ci[:, 2:3], T.ci[:, 0:1], 15, None, A.bitwise_and))
    add(s1, V.tensor_scalar(T.ci[:, 3:4], T.ci[:, 0:1], 4, 3, A.arith_shift_right, A.bitwise_and))
    z0 = group()
    for k in range(K):
        add(z0, V.memset(T["rc%d" % k][:, 0:8], 0.0))
    add(z0, V.memset(T.dm[:, 0:nd * K], 0.0))
    add(z0, V.memset(T.ct[:, :], 0.0))
    wait("V", V, s1)
    s2 = one(V.tensor_copy(T.cf[:, :], T.ci[:, :]))
    wz = group()
    vz = 512 if is_rank else TB
    add(wz, V.memset(T.win[:, 0:vz], 0.0))
    for c in range(vz, TB, 128):
        wait("S", S, it_cp)
        add(wz, S.activation(T.win[:, c:c + 128], T.colp[:, 0:128], F.Copy, scale=0.0))
    wait("V", V, s2, m0)
    s3 = group()
    add(s3, V.tensor_scalar(T.cd[:, 8:8 + K], T.ebase[:, 0:K], g4, None, A.add))
    add(s3, V.tensor_scalar(cd(0), rp, -16.0, None, A.mult))
    wait("V", V, it_cp)
    gt = one(V.tensor_scalar(T.mgt[:, :], T.colp[:, 0:128], rp, None, A.is_gt))
    mr = one(V.tensor_scalar(T.mr[:, :], T.colp[:, 0:128], rp, None, A.is_equal))
    me4 = one(V.tensor_scalar(T.me[:, :], T.colp[:, 0:EL], g4, None, A.is_equal))
    wait("V", V, it_cg)
    mb = one(V.tensor_scalar(T.mb[:, :], T.colg[:, :], rg, None, A.is_equal))
    wait("V", V, s3)
    njl = one(V.tensor_scalar(T.njl[:, :], T.colp[:, 0:128], -1.0, cd(0), A.mult, A.add))
    wait("V", V, z0)
    dmg = group()
    for k in range(K):
        add(dmg, V.memset(T.dm[0:64, nd * k + 2 * k:nd * k + 2 * k + 1], 1.0))
        add(dmg, V.memset(T.dm[64:128, nd * k + 2 * k + 1:nd * k + 2 * k + 2], 1.0))
    wait("V", V, mb, gt)
    ml = one(V.tensor_tensor(T.ml[:, :], T.mgt[:, :], T.mb[:, :], A.mult))

    s5, jt, kc = group(), group(), {}

    def consts_a():
        add(s5, V.tensor_scalar(cd(4), rp, 0.0, None, A.is_equal))
        add(s5, V.tensor_scalar(cd(5), rp, 0.0, None, A.is_gt))
        add(s5, V.tensor_scalar(cd(2), rp, 1.0, rg, A.is_equal, A.mult))
        for k in range(K):
            add(s5, V.tensor_scalar(cd(12 + k), rg, 128.0, float(1024 * k - TB), A.mult, A.add))
        wait("V", V, it_jn, mr)
        add(jt, V.tensor_scalar(T.jt[:, :], T.n16[:, 0:16], rp, None, A.add))

    def consts_b():
        wait("V", V, s5)
        for k in range(K):
            add(jt, V.tensor_scalar(T["rs%d" % k][:, :], T.colp[:, 0:16], rp, cd(12 + k), A.is_equal, A.mult))

    def consts_c():
        wt = one(V.tensor_scalar(cd(3), cd(2), 256.0, cd(4), A.mult, A.add))
        kc["va"] = one(V.tensor_scalar(T.vals[:, :], T.jnum[:, :], cd(4), cd(5), A.mult, A.add))
        wait("V", V, wt)
        kc["mz"] = one(V.tensor_scalar(T.mz[:, :], T.colp[:, 0:144], 15.0, cd(3), A.is_equal, A.mult))
    if not is_rank:
        consts_a()
        consts_b()
        consts_c()

    wait("V", V, exw)
    oh, sc, pl, mul = [], [], [], []

    def masked(k):
        wait("V", V, pl[k])
        mul.append(one(V.tensor_tensor(T["v%d" % k][:, :], T["pp%d" % k][:, 0:128], T["oh%d" % k][:, :], A.mult)))

    for k in range(K):
        oh.append(one(V.tensor_scalar(T["oh%d" % k][:, :], T.exi[:, :], cd(8 + k), None, A.is_equal)))
    for k in range(K):
        o = T["oh%d" % k]
        wait("V", V, oh[k])
        sc.append(one(V.tensor_tensor_scan(T["rc%d" % k][:, 8:136], o[:, :], o[:, :], 0.0, A.add, A.max)))
    wait("P", P, mr, njl)
    for k in range(K):
        P.matmul(T["pp%d" % k][:, 0:128], T.mr[0:16, :], T.njl[0:16, :], True, False)
    wait("P", P, mb, ml, z0)
    for k in range(K):
        o, c, pp = T["oh%d" % k], T["rc%d" % k], T["pp%d" % k]
        wait("P", P, oh[k])
        P.matmul(pp[:, 0:128], T.ml[:, :], o[:, :], False, False)
        wait("P", P, sc[k])
        pl.append(one(P.matmul(pp[:, 0:128], T.mb[:, :], c[:, 7:135], False, True)))
    rh = group()
    wait("V", V, me4)
    for k in range(K):
        wait("V", V, sc[k])
        add(rh, V.tensor_scalar(T["rh%d" % k][:, :], T.me[:, :], T["rc%d" % k][:, 135:136], None, A.mult))
    wait("P", P, dmg, rh)
    for k in range(K):
        inst = P.matmul(T.pc[0:nd, 0:EL], T.dm[:, nd * k:nd * k + nd], T["rh%d" % k][:, :], k == 0, k == K - 1)
    pc = one(inst)
    wait("S", S, pc, z0)
    ctd = one(S.activation(T.ct[0:nd, 0:EL], T.pc[0:nd, 0:EL], F.Copy))
    wait("Y", Y, ctd)
    Y.dma_start(T.cb[0:nd], T.ct[0:nd, :]).then_inc(T.sem.cbs, 16)
    if is_rank:
        Y.dma_start(T.rcnt[r], T.ct[nd - 1:nd, :]).then_inc(T.sem.own, 16)
        consts_a()
    masked(0)
    if is_rank:
        consts_b()
    for k in range(1, K):
        masked(k)
    wait("P", P, jt)
    P.matmul(T.pq[:, 0:16], T.mr[0:16, :], T.jt[0:16, :], True, False)
    for k in range(K):
        P.matmul(T.pq[:, 0:16], T["oh%d" % k][:, :], T["rs%d" % k][:, :], False, False)
    for k in range(K):
        wait("P", P, mul[k])
        inst = P.matmul(T.pq[:, 0:16], T["v%d" % k][:, :], T.mr[:, 0:16], False, k == K - 1)
    qd = one(inst)
    if is_rank:
        consts_c()
    wait("V", V, qd)
    of = one(V.tensor_scalar(T.off[:, :], T.pq[:, 0:16], float(TB), None, A.add))
    wait("V", V, of, kc["va"], wz)
    scat = one(V.tensor_copy(T.win[:, 0:TB + 256].indirect(T.off[:, 0:16]), T.vals[:, :]))
    wait("P", P, scat, kc["mz"])
    ll = []
    for k in range(K):
        for m in range(16):
            inst = P.matmul(T["pp%d" % k][:, 0:64], T.mz[:, 15 - m:143 - m], T.win[:, 1024 * k + m:1024 * (k + 1):16],
                            m == 0, m == 15)
        ll.append(one(inst))
    blk = []
    for k in range(K):
        wait("V", V, ll[k])
        lk = one(V.tensor_copy(T["list%d" % k][:, :], T["pp%d" % k][:, 0:64]))
        wait("V", V, lk, *xw)
        wait("S", S, lk, *xw)
        for i in (2 * k, 2 * k + 1):
            buf, b0 = (T.recv, r * BLK) if dests[i] == r else (T["sb%d" % i], 0)
            a = 32 * (i - 2 * k)
            two = group()
            for q in range(2):
                src = T.xs[:, :].indirect(T["list%d" % k][:, a + 16 * q:a + 16 * q + 16])
                dst = buf[:, b0 + 256 * q:b0 + 256 * q + 256]
                add(two, V.tensor_copy(dst, src) if q == 0 else S.activation(dst, src, F.Copy))
            blk.append(two)
    wait("g", g, named("cbs", 16))
    remote = [i for i in range(nd) if dests[i] != r]
    ne = cnt_engines(dests, r)
    send_fused([(cores[dests[i]], T.rcnt[r], T.cb[i], engines(topo.mask(core, cores[dests[i]]))[ne * i:ne * i + ne], T.sem.cin)
                for i in remote])
    if is_rank:
        it_pb = one(g.iota(T.pbase[0:16, :], [[CAPP, EL], [16, NP]], 0, 1, allow_small_or_imprecise_dtypes=True))
    for i in remote:
        wait("g", g, blk[i])
        if is_rank and i == 0:
            send(third, T.sb0[:, :], T.sb0[:, :], T.sem.rl, topo.mask(core, third))
        else:
            send(cores[dests[i]], landing, T["sb%d" % i][:, :], T.sem.arr, topo.mask(core, cores[dests[i]]))
    if not is_rank:
        g.wait_ge(T.sem.ls, local[0])
        return

    zz = one(V.memset(T.recv[:, ZERO:ZERO + NZ], 0.0))
    rq = T.cf[0:N, 0:1]
    cm = group()
    add(cm, V.tensor_scalar(T.mcum[:, :], T.colg[0:N, :], rq, None, A.is_ge))
    add(cm, V.tensor_scalar(T.msel[:, :], T.colg[0:N, :], rq, None, A.is_equal))
    mrf = group()
    add(mrf, V.tensor_copy(T.mrf[:, :], T.mr[:, :]))
    add(mrf, V.tensor_copy(T.mrh[:, :], T.mr[:, :]))
    pcm = one(V.tensor_scalar(T.pcmp[:, :], T.n16[:, :], rp, None, A.add))
    ncin = narr = 0
    for q in range(N):
        if q == r:
            continue
        ws, th = plan(q, cores, topo)
        for w, ds in ws:
            if r in ds:
                ncin += cnt_engines(ds, q)
                narr += len(engines(topo.mask(th if w == cores[q] and ds[0] == r else w, me)))
    Y.wait_ge(T.sem.own, 16)
    Y.wait_ge(T.sem.cin, ncin)
    Y.dma_start(T.cnts[:, :], T.rcnt[:, 0:2, :]).then_inc(T.sem.cld, 16)
    wait("P", P, it_pb, mrf, of)
    P.matmul(T.pq[:, 0:EL * NP], T.mrf[0:16, :], T.pbase[0:16, :], True, False)
    wait("P", P, named("cld", 16), cm)
    P.matmul(T.pc[:, 8:8 + EL], T.msel[:, :], T.cnts[:, :], True, True)
    cum = one(P.matmul(T.pc[:, 0:EL], T.mcum[:, :], T.cnts[:, :], True, True))
    wait("V", V, cum)
    wg = one(V.tensor_scalar(T.wgt[:, :], T.pc[:, 8:8 + EL], -1.0, float(BLK), A.mult, A.add))
    wait("V", V, wg, pcm)
    ff = group()
    for e in range(EL):
        add(ff, V.tensor_scalar(T.ff[:, NP * e:NP * e + NP], T.pcmp[:, :], T.pc[:, e:e + 1], T.wgt[:, e:e + 1],
                                A.is_ge, A.mult))
    wait("P", P, ff)
    lr = one(P.matmul(T.pq[:, 0:EL * NP], T.mrh[:, :], T.ff[:, :], False, True))
    wait("V", V, lr)
    yl = one(V.tensor_copy(T.ylist[:, :], T.pq[:, 0:EL * NP]))
    ar = named("arr", narr)
    wait("V", V, yl, ar, zz, blk[-1])
    wait("S", S, yl, ar, zz, blk[-1])
    yo = {}
    for i in range(2):
        for q, e in ((0, i), (1, 2 + i)):
            src = T.recv[:, :].indirect(T.ylist[:, NP * e:NP * e + NP])
            out = T.yt[:, CAP * e:CAP * e + CAP]
            yo[e] = one(V.tensor_copy(out, src) if q == 0 else S.activation(out, src, F.Copy))
    for e in (0, 2, 1):
        wait("Y", Y, yo[e])
        Y.dma_start(T.y[:, CAP * e:CAP * e + CAP], T.yt[:, CAP * e:CAP * e + CAP]).then_inc(T.sem.ysa, 16)
    wait("S", S, yo[3])
    S.dma_start(T.y[:, 3 * CAP:4 * CAP], T.yt[:, 3 * CAP:4 * CAP]).then_inc(T.sem.ysb, 16)
    Y.wait_ge(T.sem.ysa, 48)
    S.wait_ge(T.sem.ysb, 16)
    g.wait_ge(T.sem.ls, local[0])
